import numpy as np
import ml_dtypes


def mxq(x, axis, fmt="e4m3"):
    dtype, down = {"e4m3": (ml_dtypes.float8_e4m3fn, 7), "e5m2": (ml_dtypes.float8_e5m2, 14)}[fmt]
    v = np.moveaxis(np.asarray(x, np.float32).astype(ml_dtypes.bfloat16).astype(np.float64), axis, -1)
    blocks = v.reshape(v.shape[:-1] + (-1, 32))
    amax = np.abs(blocks).max(-1, keepdims=True)
    byte = np.maximum(np.where(amax > 0, np.frexp(amax)[1] - 1 + 127, 0) - down, 1)
    scale = np.exp2(byte - 127.0)
    codes = (blocks / scale).astype(np.float32).astype(dtype).astype(np.float64)
    return np.moveaxis((codes * scale).reshape(v.shape), -1, axis)


WIDE = False


def mx_kscale(k):
    if not WIDE:
        return np.ones(k)
    levels = np.array([10, -10, 5, -5, 0])
    if k % 512:
        return np.exp2(np.random.permutation(np.resize(levels, k // 32))).repeat(32)
    a = np.empty((k // 512, 16))
    for p in range(k // 512):
        a[p, :8] = np.random.permutation(np.resize(levels, 8))
        for g in range(8):
            far = levels[np.abs(levels - a[p, g]) >= 10]
            a[p, g + 8] = far[np.random.randint(len(far))]
    return np.exp2(a.ravel()).repeat(32)


BF16 = ml_dtypes.bfloat16


def bf(x):
    return np.asarray(x, np.float32).astype(BF16)


def f64(x):
    return np.asarray(x).astype(np.float64)


Y, X = 2048, 512
DAMP = 0.35


def setup_inputs():
    s, u = mx_kscale(X), mx_kscale(Y)
    return {"err": bf(np.random.standard_normal((Y, X)) * s * u[:, None]),
            "pre": bf(DAMP * np.random.standard_normal((X, X)) / np.sqrt(X) / s[:, None] * s),
            "coarse": bf(DAMP * np.random.standard_normal((Y, Y)) / np.sqrt(Y) / u * u[:, None]),
            "post": bf(DAMP * np.random.standard_normal((X, X)) / np.sqrt(X) / s[:, None] * s),
            "row_unscale": bf((1 + 0.1 * np.random.standard_normal(Y)) / u),
            "col_unscale": bf((1 + 0.1 * np.random.standard_normal(X)) / s)}


def reference(err, pre, coarse, post, row_unscale, col_unscale):
    e0 = f64(err)
    e1 = e0 - (mxq(e0, 1, "e4m3") @ mxq(f64(pre), 0, "e4m3"))
    cgc = mxq(f64(coarse), 1, "e4m3") @ mxq(e1, 0, "e4m3")
    e2 = f64(row_unscale)[:, None] * (e1 - cgc)
    e3 = e2 - (mxq(e2, 1, "e4m3") @ mxq(f64(post), 0, "e4m3"))
    return e3 * f64(col_unscale)

@@ -1,0 +1,333 @@
+from contextlib import ExitStack
+
+import concourse.mybir as mybir
+from concourse.masks import make_identity
+
+Y, X = 2048, 512
+FLOPS = 2 * Y * X * X + 2 * Y * Y * X + 2 * Y * X * X
+
+F32 = mybir.dt.float32
+BF16 = mybir.dt.bfloat16
+U32 = mybir.dt.uint32
+U8 = mybir.dt.uint8
+FP8X4 = mybir.dt.float8_e4m3fn_x4
+ALU = mybir.AluOpType
+ACT = mybir.ActivationFunctionType
+
+P = 128
+PACK = 4
+K_PASS = P * PACK
+GROUPS = Y // K_PASS
+TILES = Y // P
+WIDE = PACK * K_PASS
+AHEAD = 6
+
+
+def tile_semicoarsened_vcycle_error_t1_kernel(tc, err, pre, coarse, post, row_unscale, col_unscale, out):
+    nc = tc.nc
+    with ExitStack() as ctx:
+        keep = ctx.enter_context(tc.tile_pool(name="keep", bufs=1))
+        work = ctx.enter_context(tc.tile_pool(name="work", bufs=2))
+        psum = ctx.enter_context(tc.psum_pool(name="psum", bufs=1))
+
+        ident = keep.tile([P, P], F32, name="ident")
+        make_identity(nc, ident[:])
+        warm = keep.tile([P, 2], F32, name="warm")
+        nc.vector.memset(warm[:], 0.0)
+        nc.scalar.copy(out=warm[:, 0:1], in_=warm[:, 1:2])
+
+        ctx.enter_context(tc.manual_schedule())
+
+        err_sb = keep.tile([P, GROUPS, PACK, X], BF16, name="err_sb", align_bytes=64)
+        r_raw = keep.tile([P, GROUPS, PACK], BF16, name="r_raw")
+        r_col = keep.tile([P, TILES], F32, name="r_col")
+        col = keep.tile([P, X], BF16, name="col", align_bytes=64)
+        out_v = out.rearrange("(g p t) x -> g p t x", p=P, t=PACK)
+        coarse_v = coarse.rearrange("(g p t) k -> g p t k", p=P, t=PACK)
+        err_v = err.rearrange("(g p t) x -> g p t x", p=P, t=PACK)
+
+        nc.gpsimd.dma_start(out=r_raw[:], in_=row_unscale.rearrange("(g p t) -> p g t", p=P, t=PACK))
+
+        def load_weight(w, name):
+            raw = work.tile([P, PACK, X], BF16, name=name, tag="wraw", bufs=2, align_bytes=64)
+            nc.sync.dma_start(out=raw[:], in_=w.rearrange("(p j) n -> p j n", j=PACK))
+            return raw
+
+        raws = []
+
+        def load_coarse(i):
+            raw = work.tile([P, Y], BF16, name="raw", tag="raw", bufs=TILES, align_bytes=64)
+            nc.sync.dma_start(out=raw[:], in_=coarse_v[i // PACK, :, i % PACK])
+            raws.append(raw)
+
+        nc.sync.dma_start(out=err_sb[:, 0, 0:2], in_=err_v[0, :, 0:2])
+        pre_raw = load_weight(pre, "pre_raw")
+        nc.sync.dma_start(out=err_sb[:, 0, 2:4], in_=err_v[0, :, 2:4])
+        nc.sync.dma_start(out=err_sb[:, 1], in_=err_v[1])
+        load_coarse(0)
+        nc.sync.dma_start(out=err_sb[:, 2], in_=err_v[2])
+        load_coarse(1)
+        nc.sync.dma_start(out=err_sb[:, 3], in_=err_v[3])
+        for i in range(2, TILES):
+            load_coarse(i)
+            if i == 4:
+                post_raw = load_weight(post, "post_raw")
+            if i == 7:
+                nc.sync.dma_start(out=col[:], in_=col_unscale.partition_broadcast(P))
+
+        def bank_tile(tag):
+            bank = psum.tile([P, X], F32, name=tag, tag=tag, bufs=1)
+            return bank
+
+        def stepped(raw2d):
+            w = raw2d.bitcast(F32)
+            return lambda c, u: w[:, 256 * c + u : 256 * (c + 1) : 2]
+
+        def turn_half(words, b):
+            bank = psum.tile([P, 2, 2, P], F32, name="tr", tag="tr", bufs=3)
+            for c in range(2):
+                for u in range(2):
+                    nc.tensor.transpose(bank[:, c, u, :], words(2 * b + c, u), ident[:])
+            return bank
+
+        def new_il():
+            il = work.tile([P, WIDE], BF16, name="il", tag="il", bufs=8, align_bytes=64)
+            return il
+
+        def evac(bank, il, b, copy=nc.scalar.copy):
+            dst = il[:].bitcast(F32).rearrange("p (c m u) -> p c m u", c=PACK, u=2)
+            copy(out=dst[:, 2 * b : 2 * b + 2], in_=bank[:].rearrange("p c u m -> p c m u"))
+
+        def turn(words):
+            il = new_il()
+            for b in range(2):
+                evac(turn_half(words, b), il, b)
+            return il
+
+        def new_codes(tag, bufs, width):
+            codes = work.tile([P, width], U32, name=tag + "_c", tag=tag + "_c", bufs=bufs, align_bytes=64)
+            scales = work.tile([P, width], U8, name=tag + "_s", tag=tag + "_s", bufs=bufs, align_bytes=64)
+            return codes, scales
+
+        def quantise(il, q, lo, hi):
+            nc.vector.quantize_mx(out=q[0][:, lo:hi].bitcast(FP8X4), scales=q[1][:, lo:hi], in_=il[:, PACK * lo : PACK * hi])
+
+        def mx(acc, left, lcol, right, rlo, rhi, start, stop):
+            nc.tensor.matmul_mx(
+                out=acc,
+                lhsT=left[0][:, lcol : lcol + P].bitcast(FP8X4),
+                lhsT_scale=left[1][:, lcol : lcol + P],
+                rhs=right[0][:, rlo:rhi].bitcast(FP8X4),
+                rhs_scale=right[1][:, rlo:rhi],
+                start=start,
+                stop=stop,
+            )
+
+        def weave(raw, split):
+            il = new_il()
+            dst = il[:].rearrange("p (n j) -> p n j", j=PACK)
+            src = raw[:].rearrange("p j n -> p n j")
+            if split > 0:
+                nc.vector.tensor_copy(out=dst[:, 0:split], in_=src[:, 0:split])
+            if split < X:
+                nc.scalar.copy(out=dst[:, split:X], in_=src[:, split:X])
+            return il
+
+        srt = {}
+        nsort = lambda i: 4 if i < 9 else 2
+
+        def sort_words(i):
+            n = nsort(i)
+            if n and i < TILES:
+                s = work.tile([P, Y], BF16, name="srt", tag="srt", bufs=4, align_bytes=64)
+                lo = K_PASS * (PACK - n)
+                nc.scalar.copy(
+                    out=s[:, lo:Y].bitcast(F32).rearrange("p (c u k) -> p c u k", c=n, u=2),
+                    in_=raws[i][:, lo:Y].bitcast(F32).rearrange("p (c k u) -> p c u k", c=n, u=2),
+                )
+                srt[i] = s
+
+        def coarse_words(i):
+            plain = stepped(raws[i][:])
+            if i not in srt:
+                return plain
+            w = srt[i][:].bitcast(F32)
+            return lambda c, u: plain(c, u) if c < PACK - nsort(i) else w[:, 256 * c + P * u : 256 * c + P * (u + 1)]
+
+        err_il = {}
+        err_q = [new_codes("err%d" % g, 1, 512) for g in range(GROUPS)]
+        e1_q = [new_codes("e1%d" % g, 1, 512) for g in range(GROUPS)]
+        pre_q = new_codes("pre", 1, 512)
+        post_q = new_codes("post", 1, 512)
+        e1_il = {}
+        c_il = {}
+        c_q = {}
+        acc1 = {}
+        acc2 = {}
+        acc3 = {}
+
+        def err_words(g):
+            return stepped(err_sb[:, g].rearrange("p t x -> p (t x)"))
+
+        def p1(g, q):
+            acc = bank_tile(["e2t", "acc2", "acc3", "acc1"][q])
+            for t in range(PACK):
+                mx(acc[:, t * P : (t + 1) * P], err_q[g], t * P, pre_q, q * P, (q + 1) * P, True, True)
+            acc1[g, q] = acc
+
+        def make_e1(g, q):
+            if q == 0:
+                e1_il[g] = work.tile([P, WIDE], BF16, name="e1il", tag="e1il", bufs=2, align_bytes=64)
+            cols = slice(q * P, (q + 1) * P)
+            nc.vector.tensor_tensor(
+                out=e1_il[g][:].rearrange("p (x t) -> p x t", t=PACK)[:, cols],
+                in0=err_sb[:, g, :, cols].rearrange("p t x -> p x t"),
+                in1=acc1[g, q][:].rearrange("p (t x) -> p x t", t=PACK),
+                op=ALU.subtract,
+            )
+
+        def quantise_c(i):
+            c_q[i] = new_codes("cq", 4, 512)
+            quantise(c_il[i], c_q[i], 0, 512)
+
+        def p2(i, c):
+            if c < 0:
+                acc2[i] = bank_tile("acc%d" % (i % 2))
+                mx(acc2[i][:], err_q[i // PACK], (i % PACK) * P, pre_q, 0, X, True, False)
+            else:
+                mx(acc2[i][:], c_q[i], c * P, e1_q[c], 0, X, False, c == GROUPS - 1)
+
+        err_il[0] = new_il()
+        evac(turn_half(err_words(0), 0), err_il[0], 0)
+        pre_il = weave(pre_raw, 320)
+        quantise(err_il[0], err_q[0], 0, 256)
+        quantise(pre_il, pre_q, 0, 512)
+        evac(turn_half(err_words(0), 1), err_il[0], 1)
+        quantise(err_il[0], err_q[0], 256, 512)
+        nc.vector.tensor_copy(out=r_col[:], in_=r_raw[:].rearrange("p g t -> p (g t)"))
+        for q in range(PACK):
+            p1(0, q)
+        turns = [[0], [1], [2, 3], [4, 5]]
+        sort_at = {1: [6], 2: [7], 3: [8]}
+        err_il[1] = turn(err_words(1))
+        for g in range(GROUPS):
+            for q in range(PACK):
+                make_e1(g, q)
+            if g + 1 < GROUPS:
+                if g < 2:
+                    quantise(err_il[g + 1], err_q[g + 1], 0, 256)
+                    quantise(err_il[g + 1], err_q[g + 1], 256, 512)
+                else:
+                    quantise(err_il[g + 1], err_q[g + 1], 0, 512)
+            if g + 2 < GROUPS:
+                err_il[g + 2] = turn(err_words(g + 2))
+            for i in turns[g]:
+                c_il[i] = turn(coarse_words(i))
+            for i in sort_at.get(g, []):
+                sort_words(i)
+            if g + 1 < GROUPS:
+                for q in range(PACK):
+                    p1(g + 1, q)
+                quantise(e1_il[g], e1_q[g], 0, 512)
+            if g == GROUPS - 2:
+                quantise_c(0)
+            if g == GROUPS - 1:
+                quantise(e1_il[g], e1_q[g], 0, 512)
+                p2(0, -1)
+                for c in range(PACK):
+                    p2(0, c)
+                quantise_c(1)
+
+        d = {}
+        e2_bf = {}
+        e2_il = {}
+        e2_q = {}
+        e3 = {}
+
+        def live(i):
+            return 0 <= i < TILES
+
+        def make_d(i):
+            dt = work.tile([P, X], F32, name="d", tag="d", bufs=6, align_bytes=64)
+            g, t = divmod(i, PACK)
+            nc.vector.tensor_tensor(out=dt[:], in0=err_sb[:, g, t], in1=acc2[i][:], op=ALU.subtract)
+            d[i] = dt
+
+        def make_e2(i):
+            eb = work.tile([P, X], BF16, name="e2b", tag="e2b", bufs=3, align_bytes=64)
+            nc.scalar.activation(
+                out=eb[:].rearrange("m (u p e) -> m u p e", u=2, e=2),
+                in_=d[i][:].rearrange("m (p u e) -> m u p e", u=2, e=2),
+                func=ACT.Copy,
+                scale=r_col[:, i : i + 1],
+            )
+            e2_bf[i] = eb
+
+        def turn_e2(i):
+            bank = bank_tile("e2t")
+            words = e2_bf[i][:].bitcast(F32)
+            for u in range(2):
+                nc.tensor.transpose(bank[:, u * P : (u + 1) * P], words[:, u * P : (u + 1) * P], ident[:])
+            il = work.tile([P, X], BF16, name="e2il", tag="e2il", bufs=2, align_bytes=64)
+            nc.scalar.copy(
+                out=il[:].bitcast(F32).rearrange("p (m u) -> p m u", u=2),
+                in_=bank[:, 0 : 2 * P].rearrange("p (u m) -> p m u", u=2),
+            )
+            e2_il[i] = il
+
+        def quantise_e2(i):
+            e2_q[i] = new_codes("e2", 3, P)
+            quantise(e2_il[i], e2_q[i], 0, P)
+
+        def p3(i):
+            acc3[i] = bank_tile("acc%d" % (2 + i % 2))
+            mx(acc3[i][:], e2_q[i], 0, post_q, 0, X, True, True)
+
+        def make_e3(i):
+            o = work.tile([P, X], F32, name="e3", tag="e3", bufs=3, align_bytes=64)
+            nc.vector.scalar_tensor_tensor(
+                out=o[:], in0=d[i][:], scalar=r_col[:, i : i + 1], in1=acc3[i][:], op0=ALU.mult, op1=ALU.subtract
+            )
+            e3[i] = o
+
+        def finish(i):
+            res = work.tile([P, X], F32, name="res", tag="res", bufs=4, align_bytes=64)
+            eng = nc.gpsimd if i in () else nc.vector
+            eng.tensor_tensor(out=res[:], in0=e3[i][:], in1=col[:], op=ALU.mult)
+            g, t = divmod(i, PACK)
+            nc.sync.dma_start(out=out_v[g, :, t], in_=res[:])
+
+        for i in range(1, TILES + 5):
+            n = i + AHEAD - 1
+            if live(i - 1):
+                make_d(i - 1)
+            if live(i - 1):
+                make_e2(i - 1)
+            if live(i + 1):
+                quantise_c(i + 1)
+            if live(i - 4):
+                make_e3(i - 4)
+            ev_v = n in ()
+            if live(n):
+                c_il[n] = new_il()
+                words = coarse_words(n)
+                evac(turn_half(words, 0), c_il[n], 0)
+            if live(i - 2):
+                turn_e2(i - 2)
+            if live(n):
+                evac(turn_half(words, 1), c_il[n], 1, nc.vector.tensor_copy if ev_v else nc.scalar.copy)
+            if live(n + 1) and n + 1 not in srt:
+                sort_words(n + 1)
+            if i == 2:
+                post_il = weave(post_raw, X)
+            if live(i - 5):
+                finish(i - 5)
+            if live(i - 2):
+                quantise_e2(i - 2)
+            if i == 3:
+                quantise(post_il, post_q, 0, 512)
+            if live(i):
+                for c in range(-1, GROUPS):
+                    p2(i, c)
+            if live(i - 3):
+                p3(i - 3)

@@ -20,7 +20,6 @@ K_PASS = P * PACK
 GROUPS = Y // K_PASS
 TILES = Y // P
 WIDE = PACK * K_PASS
-AHEAD = 6
 
 
 def tile_semicoarsened_vcycle_error_t1_kernel(tc, err, pre, coarse, post, row_unscale, col_unscale, out):
@@ -39,6 +38,7 @@ def tile_semicoarsened_vcycle_error_t1_kernel(tc, err, pre, coarse, post, row_un
         ctx.enter_context(tc.manual_schedule())
 
         err_sb = keep.tile([P, GROUPS, PACK, X], BF16, name="err_sb", align_bytes=64)
+        e1 = keep.tile([P, GROUPS, PACK, X], F32, name="e1", align_bytes=64)
         r_raw = keep.tile([P, GROUPS, PACK], BF16, name="r_raw")
         r_col = keep.tile([P, TILES], F32, name="r_col")
         col = keep.tile([P, X], BF16, name="col", align_bytes=64)
@@ -46,17 +46,15 @@ def tile_semicoarsened_vcycle_error_t1_kernel(tc, err, pre, coarse, post, row_un
         coarse_v = coarse.rearrange("(g p t) k -> g p t k", p=P, t=PACK)
         err_v = err.rearrange("(g p t) x -> g p t x", p=P, t=PACK)
 
-        nc.gpsimd.dma_start(out=r_raw[:], in_=row_unscale.rearrange("(g p t) -> p g t", p=P, t=PACK))
-
         def load_weight(w, name):
-            raw = work.tile([P, PACK, X], BF16, name=name, tag="wraw", bufs=2, align_bytes=64)
+            raw = work.tile([P, PACK, X], BF16, name=name, tag="raw", bufs=16, align_bytes=64)
             nc.sync.dma_start(out=raw[:], in_=w.rearrange("(p j) n -> p j n", j=PACK))
             return raw
 
         raws = []
 
         def load_coarse(i):
-            raw = work.tile([P, Y], BF16, name="raw", tag="raw", bufs=TILES, align_bytes=64)
+            raw = work.tile([P, Y], BF16, name="raw", tag="raw", bufs=16, align_bytes=64)
             nc.sync.dma_start(out=raw[:], in_=coarse_v[i // PACK, :, i % PACK])
             raws.append(raw)
 
@@ -68,266 +66,244 @@ def tile_semicoarsened_vcycle_error_t1_kernel(tc, err, pre, coarse, post, row_un
         nc.sync.dma_start(out=err_sb[:, 2], in_=err_v[2])
         load_coarse(1)
         nc.sync.dma_start(out=err_sb[:, 3], in_=err_v[3])
-        for i in range(2, TILES):
-            load_coarse(i)
-            if i == 4:
-                post_raw = load_weight(post, "post_raw")
-            if i == 7:
-                nc.sync.dma_start(out=col[:], in_=col_unscale.partition_broadcast(P))
+        load_coarse(2)
+        load_coarse(3)
+        nc.sync.dma_start(out=r_raw[:], in_=row_unscale.rearrange("(g p t) -> p g t", p=P, t=PACK))
+        load_coarse(4)
+        post_raw = load_weight(post, "post_raw")
+        load_coarse(5)
+        load_coarse(6)
+        load_coarse(7)
+        nc.sync.dma_start(out=col[:], in_=col_unscale.partition_broadcast(P))
+        load_coarse(8)
+        load_coarse(9)
+        load_coarse(10)
+        load_coarse(11)
+        load_coarse(12)
+        load_coarse(13)
+
 
         def bank_tile(tag):
             bank = psum.tile([P, X], F32, name=tag, tag=tag, bufs=1)
             return bank
 
-        def stepped(raw2d):
-            w = raw2d.bitcast(F32)
-            return lambda c, u: w[:, 256 * c + u : 256 * (c + 1) : 2]
-
-        def turn_half(words, b):
-            bank = psum.tile([P, 2, 2, P], F32, name="tr", tag="tr", bufs=3)
-            for c in range(2):
-                for u in range(2):
-                    nc.tensor.transpose(bank[:, c, u, :], words(2 * b + c, u), ident[:])
-            return bank
-
-        def new_il():
-            il = work.tile([P, WIDE], BF16, name="il", tag="il", bufs=8, align_bytes=64)
-            return il
-
-        def evac(bank, il, b, copy=nc.scalar.copy):
-            dst = il[:].bitcast(F32).rearrange("p (c m u) -> p c m u", c=PACK, u=2)
-            copy(out=dst[:, 2 * b : 2 * b + 2], in_=bank[:].rearrange("p c u m -> p c m u"))
-
-        def turn(words):
-            il = new_il()
-            for b in range(2):
-                evac(turn_half(words, b), il, b)
-            return il
+        nsort = lambda i: 2 if i > 2 else 0
+        tr = {}
+        il = {}
+        srt = {}
+        q = {}
+        acc = {}
+        d = {}
+        e2b = {}
+        e3 = {}
+        state = {"p1": 0, "p3": 0, "late": 14}
 
         def new_codes(tag, bufs, width):
             codes = work.tile([P, width], U32, name=tag + "_c", tag=tag + "_c", bufs=bufs, align_bytes=64)
             scales = work.tile([P, width], U8, name=tag + "_s", tag=tag + "_s", bufs=bufs, align_bytes=64)
             return codes, scales
 
-        def quantise(il, q, lo, hi):
-            nc.vector.quantize_mx(out=q[0][:, lo:hi].bitcast(FP8X4), scales=q[1][:, lo:hi], in_=il[:, PACK * lo : PACK * hi])
+        def quantise(src, dst, lo, hi):
+            nc.vector.quantize_mx(out=dst[0][:, lo:hi].bitcast(FP8X4), scales=dst[1][:, lo:hi], in_=src[:, PACK * lo : PACK * hi])
 
-        def mx(acc, left, lcol, right, rlo, rhi, start, stop):
+        def mx(out_ap, left, lcol, right, start, stop):
             nc.tensor.matmul_mx(
-                out=acc,
+                out=out_ap,
                 lhsT=left[0][:, lcol : lcol + P].bitcast(FP8X4),
                 lhsT_scale=left[1][:, lcol : lcol + P],
-                rhs=right[0][:, rlo:rhi].bitcast(FP8X4),
-                rhs_scale=right[1][:, rlo:rhi],
+                rhs=right[0][:].bitcast(FP8X4),
+                rhs_scale=right[1][:],
                 start=start,
                 stop=stop,
             )
 
-        def weave(raw, split):
-            il = new_il()
-            dst = il[:].rearrange("p (n j) -> p n j", j=PACK)
-            src = raw[:].rearrange("p j n -> p n j")
-            if split > 0:
-                nc.vector.tensor_copy(out=dst[:, 0:split], in_=src[:, 0:split])
-            if split < X:
-                nc.scalar.copy(out=dst[:, split:X], in_=src[:, split:X])
-            return il
+        def turn(key, words):
+            bank = psum.tile([P, 2, 2, P], F32, name="tr", tag="tr", bufs=3)
+            for c in range(2):
+                for u in range(2):
+                    nc.tensor.transpose(bank[:, c, u, :], words(c, u), ident[:])
+            tr[key] = bank
 
-        srt = {}
-        nsort = lambda i: 4 if i < 9 else 2
+        def untangle(key, il_key, b, copy):
+            if il_key not in il:
+                il[il_key] = work.tile([P, WIDE], BF16, name="il", tag="il", bufs=7, align_bytes=64)
+            dst = il[il_key][:].bitcast(F32).rearrange("p (c m u) -> p c m u", c=PACK, u=2)
+            copy(out=dst[:, 2 * b : 2 * b + 2], in_=tr[key][:].rearrange("p c u m -> p c m u"))
 
-        def sort_words(i):
-            n = nsort(i)
-            if n and i < TILES:
-                s = work.tile([P, Y], BF16, name="srt", tag="srt", bufs=4, align_bytes=64)
-                lo = K_PASS * (PACK - n)
+        def weave(key, raw, lo, hi, copy):
+            if key not in il:
+                il[key] = work.tile([P, WIDE], BF16, name="il", tag="il", bufs=7, align_bytes=64)
+            copy(
+                out=il[key][:].rearrange("p (n j) -> p n j", j=PACK)[:, lo:hi],
+                in_=raw[:].rearrange("p j n -> p n j")[:, lo:hi],
+            )
+
+        def weave_e1(g, lo, hi, copy):
+            key = "e1", g
+            if key not in il:
+                il[key] = work.tile([P, WIDE], BF16, name="e1il", tag="e1il", bufs=2, align_bytes=64)
+            copy(
+                out=il[key][:].rearrange("p (x t) -> p x t", t=PACK)[:, lo:hi],
+                in_=e1[:, g].rearrange("p t x -> p x t")[:, lo:hi],
+            )
+
+        def step(tok):
+            k = tok.split()
+            n = [int(v) for v in k[1:]]
+            k = k[0]
+            i = n[0] if n else 0
+            if k == "E":
+                w = err_sb[:, i].rearrange("p t x -> p (t x)").bitcast(F32)
+                turn(("e", i, n[1]), lambda c, u: w[:, 512 * n[1] + 256 * c + u : 512 * n[1] + 256 * (c + 1) : 2])
+            elif k == "e":
+                untangle(("e", i, n[1]), ("e", i), n[1], nc.scalar.copy)
+            elif k == "C":
+                w = raws[i][:].bitcast(F32)
+                first = PACK - nsort(i)
+
+                def words(c, u):
+                    c = 2 * n[1] + c
+                    if c < first:
+                        return w[:, 256 * c + u : 256 * (c + 1) : 2]
+                    s = srt[i][:].bitcast(F32)
+                    return s[:, 256 * (c - first) + P * u : 256 * (c - first) + P * (u + 1)]
+
+                turn(("c", i, n[1]), words)
+            elif k == "c":
+                untangle(("c", i, n[1]), ("c", i), n[1], nc.scalar.copy)
+            elif k == "cv":
+                untangle(("c", i, n[1]), ("c", i), n[1], nc.vector.tensor_copy)
+            elif k == "s":
+                m = nsort(i)
+                lo = K_PASS * (PACK - m)
+                srt[i] = work.tile([P, K_PASS * m], BF16, name="srt", tag="srt", bufs=3, align_bytes=64)
                 nc.scalar.copy(
-                    out=s[:, lo:Y].bitcast(F32).rearrange("p (c u k) -> p c u k", c=n, u=2),
-                    in_=raws[i][:, lo:Y].bitcast(F32).rearrange("p (c k u) -> p c u k", c=n, u=2),
+                    out=srt[i][:].bitcast(F32).rearrange("p (c u k) -> p c u k", c=m, u=2),
+                    in_=raws[i][:, lo:Y].bitcast(F32).rearrange("p (c k u) -> p c u k", c=m, u=2),
                 )
-                srt[i] = s
-
-        def coarse_words(i):
-            plain = stepped(raws[i][:])
-            if i not in srt:
-                return plain
-            w = srt[i][:].bitcast(F32)
-            return lambda c, u: plain(c, u) if c < PACK - nsort(i) else w[:, 256 * c + P * u : 256 * c + P * (u + 1)]
-
-        err_il = {}
-        err_q = [new_codes("err%d" % g, 1, 512) for g in range(GROUPS)]
-        e1_q = [new_codes("e1%d" % g, 1, 512) for g in range(GROUPS)]
-        pre_q = new_codes("pre", 1, 512)
-        post_q = new_codes("post", 1, 512)
-        e1_il = {}
-        c_il = {}
-        c_q = {}
-        acc1 = {}
-        acc2 = {}
-        acc3 = {}
-
-        def err_words(g):
-            return stepped(err_sb[:, g].rearrange("p t x -> p (t x)"))
-
-        def p1(g, q):
-            acc = bank_tile(["e2t", "acc2", "acc3", "acc1"][q])
-            for t in range(PACK):
-                mx(acc[:, t * P : (t + 1) * P], err_q[g], t * P, pre_q, q * P, (q + 1) * P, True, True)
-            acc1[g, q] = acc
-
-        def make_e1(g, q):
-            if q == 0:
-                e1_il[g] = work.tile([P, WIDE], BF16, name="e1il", tag="e1il", bufs=2, align_bytes=64)
-            cols = slice(q * P, (q + 1) * P)
-            nc.vector.tensor_tensor(
-                out=e1_il[g][:].rearrange("p (x t) -> p x t", t=PACK)[:, cols],
-                in0=err_sb[:, g, :, cols].rearrange("p t x -> p x t"),
-                in1=acc1[g, q][:].rearrange("p (t x) -> p x t", t=PACK),
-                op=ALU.subtract,
-            )
-
-        def quantise_c(i):
-            c_q[i] = new_codes("cq", 4, 512)
-            quantise(c_il[i], c_q[i], 0, 512)
-
-        def p2(i, c):
-            if c < 0:
-                acc2[i] = bank_tile("acc%d" % (i % 2))
-                mx(acc2[i][:], err_q[i // PACK], (i % PACK) * P, pre_q, 0, X, True, False)
-            else:
-                mx(acc2[i][:], c_q[i], c * P, e1_q[c], 0, X, False, c == GROUPS - 1)
-
-        err_il[0] = new_il()
-        evac(turn_half(err_words(0), 0), err_il[0], 0)
-        pre_il = weave(pre_raw, 320)
-        quantise(err_il[0], err_q[0], 0, 256)
-        quantise(pre_il, pre_q, 0, 512)
-        evac(turn_half(err_words(0), 1), err_il[0], 1)
-        quantise(err_il[0], err_q[0], 256, 512)
-        nc.vector.tensor_copy(out=r_col[:], in_=r_raw[:].rearrange("p g t -> p (g t)"))
-        for q in range(PACK):
-            p1(0, q)
-        turns = [[0], [1], [2, 3], [4, 5]]
-        sort_at = {1: [6], 2: [7], 3: [8]}
-        err_il[1] = turn(err_words(1))
-        for g in range(GROUPS):
-            for q in range(PACK):
-                make_e1(g, q)
-            if g + 1 < GROUPS:
-                if g < 2:
-                    quantise(err_il[g + 1], err_q[g + 1], 0, 256)
-                    quantise(err_il[g + 1], err_q[g + 1], 256, 512)
+            elif k == "wV":
+                weave("pre", pre_raw, 0, 320, nc.vector.tensor_copy)
+            elif k == "wS":
+                weave("pre", pre_raw, 320, X, nc.scalar.copy)
+            elif k == "pre":
+                q["pre"] = new_codes("pre", 1, 512)
+                quantise(il["pre"], q["pre"], 0, 512)
+            elif k == "wp":
+                weave("post", post_raw, 0, X, nc.vector.tensor_copy)
+            elif k == "postq":
+                q["post"] = new_codes("post", 1, 512)
+                quantise(il["post"], q["post"], 0, 512)
+            elif k == "h":
+                if ("e", i) not in q:
+                    q["e", i] = new_codes("err", 2, 512)
+                if i < 2:
+                    quantise(il["e", i], q["e", i], 256 * n[1], 256 * (n[1] + 1))
                 else:
-                    quantise(err_il[g + 1], err_q[g + 1], 0, 512)
-            if g + 2 < GROUPS:
-                err_il[g + 2] = turn(err_words(g + 2))
-            for i in turns[g]:
-                c_il[i] = turn(coarse_words(i))
-            for i in sort_at.get(g, []):
-                sort_words(i)
-            if g + 1 < GROUPS:
-                for q in range(PACK):
-                    p1(g + 1, q)
-                quantise(e1_il[g], e1_q[g], 0, 512)
-            if g == GROUPS - 2:
-                quantise_c(0)
-            if g == GROUPS - 1:
-                quantise(e1_il[g], e1_q[g], 0, 512)
-                p2(0, -1)
-                for c in range(PACK):
-                    p2(0, c)
-                quantise_c(1)
+                    quantise(il["e", i], q["e", i], 0, 512)
+            elif k == "P":
+                bank = bank_tile(["e2t", "acc2", "acc3"][state["p1"] % 3])
+                state["p1"] += 1
+                mx(bank[:], q["e", i], n[1] * P, q["pre"], True, True)
+                acc["e", i, n[1]] = bank
+            elif k == "t":
+                nc.vector.tensor_tensor(out=e1[:, i, n[1]], in0=err_sb[:, i, n[1]], in1=acc["e", i, n[1]][:], op=ALU.subtract)
+            elif k == "iS":
+                weave_e1(i, 0, 448 if i < 3 else 192, nc.scalar.copy)
+            elif k == "iV":
+                weave_e1(i, 448 if i < 3 else 192, X, nc.vector.tensor_copy)
+            elif k == "q1":
+                q["1", i] = new_codes("e1%d" % i, 1, 512)
+                quantise(il["e1", i], q["1", i], 0, 512)
+            elif k == "R":
+                nc.vector.tensor_copy(out=r_col[:], in_=r_raw[:].rearrange("p g t -> p (g t)"))
+            elif k == "qc":
+                q["c", i] = new_codes("cq", 4, 512)
+                quantise(il["c", i], q["c", i], 0, 512)
+            elif k == "2":
+                if n[1] == 0:
+                    acc[i] = bank_tile("acc%d" % (i % 2))
+                mx(acc[i][:], q["c", i], n[1] * P, q["1", n[1]], n[1] == 0, n[1] == 3)
+            elif k == "d":
+                d[i] = work.tile([P, X], F32, name="d", tag="d", bufs=6, align_bytes=64)
+                nc.vector.tensor_tensor(out=d[i][:], in0=e1[:, i // PACK, i % PACK], in1=acc[i][:], op=ALU.subtract)
+            elif k == "b":
+                e2b[i] = work.tile([P, X], BF16, name="e2b", tag="e2b", bufs=3, align_bytes=64)
+                nc.scalar.activation(
+                    out=e2b[i][:].rearrange("m (u p e) -> m u p e", u=2, e=2),
+                    in_=d[i][:].rearrange("m (p u e) -> m u p e", u=2, e=2),
+                    func=ACT.Copy,
+                    scale=r_col[:, i : i + 1],
+                )
+            elif k == "T":
+                bank = bank_tile("e2t")
+                w = e2b[i][:].bitcast(F32)
+                for u in range(2):
+                    nc.tensor.transpose(bank[:, u * P : (u + 1) * P], w[:, u * P : (u + 1) * P], ident[:])
+                tr["e2", i] = bank
+            elif k == "x":
+                il["e2", i] = work.tile([P, X], BF16, name="e2il", tag="e2il", bufs=2, align_bytes=64)
+                nc.scalar.copy(
+                    out=il["e2", i][:].bitcast(F32).rearrange("p (m u) -> p m u", u=2),
+                    in_=tr["e2", i][:, 0 : 2 * P].rearrange("p (u m) -> p m u", u=2),
+                )
+            elif k == "y":
+                q["e2", i] = new_codes("e2", 3, P)
+                quantise(il["e2", i], q["e2", i], 0, P)
+            elif k == "3":
+                acc["3", i] = bank_tile("acc%d" % (2 + i % 2))
+                mx(acc["3", i][:], q["e2", i], 0, q["post"], True, True)
+            elif k == "z":
+                e3[i] = work.tile([P, X], F32, name="e3", tag="e3", bufs=3, align_bytes=64)
+                nc.vector.scalar_tensor_tensor(
+                    out=e3[i][:], in0=d[i][:], scalar=r_col[:, i : i + 1], in1=acc["3", i][:], op0=ALU.mult, op1=ALU.subtract
+                )
+            elif k in ("f", "fp"):
+                res = work.tile([P, X], F32, name="res", tag="res", bufs=4, align_bytes=64)
+                eng = nc.vector if k == "f" else nc.gpsimd
+                eng.tensor_tensor(out=res[:], in0=e3[i][:], in1=col[:], op=ALU.mult)
+                nc.sync.dma_start(out=out_v[i // PACK, :, i % PACK], in_=res[:])
+            elif k == "L":
+                load_coarse(i)
+            else:
+                raise AssertionError(tok)
 
-        d = {}
-        e2_bf = {}
-        e2_il = {}
-        e2_q = {}
-        e3 = {}
-
-        def live(i):
-            return 0 <= i < TILES
-
-        def make_d(i):
-            dt = work.tile([P, X], F32, name="d", tag="d", bufs=6, align_bytes=64)
-            g, t = divmod(i, PACK)
-            nc.vector.tensor_tensor(out=dt[:], in0=err_sb[:, g, t], in1=acc2[i][:], op=ALU.subtract)
-            d[i] = dt
-
-        def make_e2(i):
-            eb = work.tile([P, X], BF16, name="e2b", tag="e2b", bufs=3, align_bytes=64)
-            nc.scalar.activation(
-                out=eb[:].rearrange("m (u p e) -> m u p e", u=2, e=2),
-                in_=d[i][:].rearrange("m (p u e) -> m u p e", u=2, e=2),
-                func=ACT.Copy,
-                scale=r_col[:, i : i + 1],
-            )
-            e2_bf[i] = eb
-
-        def turn_e2(i):
-            bank = bank_tile("e2t")
-            words = e2_bf[i][:].bitcast(F32)
-            for u in range(2):
-                nc.tensor.transpose(bank[:, u * P : (u + 1) * P], words[:, u * P : (u + 1) * P], ident[:])
-            il = work.tile([P, X], BF16, name="e2il", tag="e2il", bufs=2, align_bytes=64)
-            nc.scalar.copy(
-                out=il[:].bitcast(F32).rearrange("p (m u) -> p m u", u=2),
-                in_=bank[:, 0 : 2 * P].rearrange("p (u m) -> p m u", u=2),
-            )
-            e2_il[i] = il
-
-        def quantise_e2(i):
-            e2_q[i] = new_codes("e2", 3, P)
-            quantise(e2_il[i], e2_q[i], 0, P)
-
-        def p3(i):
-            acc3[i] = bank_tile("acc%d" % (2 + i % 2))
-            mx(acc3[i][:], e2_q[i], 0, post_q, 0, X, True, True)
-
-        def make_e3(i):
-            o = work.tile([P, X], F32, name="e3", tag="e3", bufs=3, align_bytes=64)
-            nc.vector.scalar_tensor_tensor(
-                out=o[:], in0=d[i][:], scalar=r_col[:, i : i + 1], in1=acc3[i][:], op0=ALU.mult, op1=ALU.subtract
-            )
-            e3[i] = o
-
-        def finish(i):
-            res = work.tile([P, X], F32, name="res", tag="res", bufs=4, align_bytes=64)
-            eng = nc.gpsimd if i in () else nc.vector
-            eng.tensor_tensor(out=res[:], in0=e3[i][:], in1=col[:], op=ALU.mult)
-            g, t = divmod(i, PACK)
-            nc.sync.dma_start(out=out_v[g, :, t], in_=res[:])
-
-        for i in range(1, TILES + 5):
-            n = i + AHEAD - 1
-            if live(i - 1):
-                make_d(i - 1)
-            if live(i - 1):
-                make_e2(i - 1)
-            if live(i + 1):
-                quantise_c(i + 1)
-            if live(i - 4):
-                make_e3(i - 4)
-            ev_v = n in ()
-            if live(n):
-                c_il[n] = new_il()
-                words = coarse_words(n)
-                evac(turn_half(words, 0), c_il[n], 0)
-            if live(i - 2):
-                turn_e2(i - 2)
-            if live(n):
-                evac(turn_half(words, 1), c_il[n], 1, nc.vector.tensor_copy if ev_v else nc.scalar.copy)
-            if live(n + 1) and n + 1 not in srt:
-                sort_words(n + 1)
-            if i == 2:
-                post_il = weave(post_raw, X)
-            if live(i - 5):
-                finish(i - 5)
-            if live(i - 2):
-                quantise_e2(i - 2)
-            if i == 3:
-                quantise(post_il, post_q, 0, 512)
-            if live(i):
-                for c in range(-1, GROUPS):
-                    p2(i, c)
-            if live(i - 3):
-                p3(i - 3)
+        for line in [
+            "E 0 0, wV, wS, L 14, E 0 1, e 0 0, e 0 1, E 1 1, h 0 0, h 0 1",
+            "E 1 0, pre, e 1 1, h 1 1, P 0 0, e 1 0, P 0 1, t 0 0, P 0 3, h 1 0",
+            "t 0 1, P 0 2, E 2 1, t 0 2, t 0 3, E 2 0, e 2 1, iV 0, P 1 3, e 2 0",
+            "P 1 2, t 1 3, C 0 1, iS 0, h 2 0, P 1 1, t 1 2, P 1 0, C 0 0, L 15",
+            "t 1 1, P 2 1, t 1 0, c 0 0, P 2 3, E 3 0, t 2 1, c 0 1, q1 0, E 3 1",
+            "e 3 0, qc 0, P 2 0, e 3 1, C 1 1, t 2 3, iS 1, h 3 0, P 2 2, 2 0 0",
+            "t 2 0, P 3 3, iV 1, P 3 2, t 2 2, C 1 0, t 3 3, c 1 1, C 2 0, t 3 2",
+            "c 1 0, P 3 1, q1 1, iS 2, P 3 0, C 2 1, t 3 1, 2 0 1, t 3 0, R",
+            "qc 1, iS 3, iV 2, iV 3, 2 1 0, 2 1 1, c 2 1, q1 2, c 2 0, q1 3",
+            "2 1 2, s 3, 2 0 2, 2 0 3, s 4, 2 1 3, d 0, C 3 1, C 3 0, qc 2",
+            "b 0, C 4 1, d 1, c 3 1, T 0, 2 2 0, c 3 0, 2 2 1, x 0, qc 3",
+            "2 2 2, s 5, 2 2 3, wp, b 1, C 4 0, c 4 1, C 5 1, postq, c 4 0",
+            "T 1, 2 3 0, y 0, x 1, d 2, 2 3 1, s 6, 2 3 2, qc 4, 2 3 3",
+            "b 2, 3 0, y 1, C 5 0, d 3, c 5 1, z 0, C 6 1, c 5 0, T 2",
+            "2 4 0, x 2, qc 5, 2 4 1, s 7, 2 4 2, y 2, 2 4 3, b 3, 3 1",
+            "d 4, C 6 0, c 6 1, z 1, C 7 1, c 6 0, T 3, f 0, 2 5 0, x 3",
+            "2 5 1, qc 6, s 8, 2 5 2, 2 5 3, y 3, b 4, 3 2, d 5, C 7 0",
+            "c 7 1, z 2, C 8 1, c 7 0, T 4, f 1, 2 6 0, x 4, 2 6 1, qc 7",
+            "s 9, 2 6 2, 2 6 3, y 4, b 5, 3 3, d 6, C 8 0, c 8 1, z 3",
+            "C 9 1, c 8 0, T 5, f 2, 2 7 0, x 5, 2 7 1, qc 8, s 10, 2 7 2",
+            "2 7 3, y 5, b 6, 3 4, d 7, C 9 0, c 9 1, z 4, C 10 1, c 9 0",
+            "T 6, f 3, 2 8 0, x 6, 2 8 1, qc 9, s 11, 2 8 2, 2 8 3, y 6",
+            "b 7, 3 5, d 8, C 10 0, c 10 1, z 5, C 11 1, c 10 0, T 7, f 4",
+            "2 9 0, x 7, 2 9 1, qc 10, s 12, 2 9 2, 2 9 3, y 7, b 8, 3 6",
+            "d 9, C 11 0, c 11 1, z 6, C 12 1, c 11 0, T 8, f 5, 2 10 0, x 8",
+            "2 10 1, qc 11, s 13, 2 10 2, 2 10 3, y 8, b 9, 3 7, d 10, C 12 0",
+            "c 12 1, z 7, C 13 1, c 12 0, T 9, f 6, 2 11 0, x 9, 2 11 1, qc 12",
+            "s 14, 2 11 2, 2 11 3, y 9, b 10, 3 8, d 11, C 13 0, c 13 1, z 8",
+            "C 14 1, c 13 0, T 10, f 7, 2 12 0, x 10, 2 12 1, qc 13, s 15, 2 12 2",
+            "2 12 3, y 10, b 11, 3 9, d 12, C 14 0, c 14 1, z 9, C 15 1, c 14 0",
+            "T 11, f 8, 2 13 0, x 11, 2 13 1, qc 14, b 12, 2 13 2, 2 13 3, y 11",
+            "c 15 1, 3 10, d 13, C 15 0, z 10, T 12, c 15 0, 2 14 0, f 9, 2 14 1",
+            "x 12, 2 14 2, qc 15, b 13, 2 14 3, 3 11, y 12, d 14, T 13, 2 15 0",
+            "z 11, x 13, 2 15 1, b 14, 2 15 2, f 10, 2 15 3, 3 12, y 13, d 15",
+            "T 14, 3 13, x 14, z 12, b 15, f 11, T 15, y 14, z 13, 3 14",
+            "x 15, f 12, y 15, z 14, 3 15, f 13, z 15, f 14, f 15",
+        ]:
+            for tok in line.split(", "):
+                step(tok)

from contextlib import ExitStack

import concourse.mybir as mybir
from concourse.masks import make_identity

Y, X = 2048, 512
FLOPS = 2 * Y * X * X + 2 * Y * Y * X + 2 * Y * X * X

F32 = mybir.dt.float32
BF16 = mybir.dt.bfloat16
U32 = mybir.dt.uint32
U8 = mybir.dt.uint8
FP8X4 = mybir.dt.float8_e4m3fn_x4
ALU = mybir.AluOpType
ACT = mybir.ActivationFunctionType

P = 128
PACK = 4
K_PASS = P * PACK
GROUPS = Y // K_PASS
TILES = Y // P
WIDE = PACK * K_PASS


def tile_semicoarsened_vcycle_error_t1_kernel(tc, err, pre, coarse, post, row_unscale, col_unscale, out):
    nc = tc.nc
    with ExitStack() as ctx:
        keep = ctx.enter_context(tc.tile_pool(name="keep", bufs=1))
        work = ctx.enter_context(tc.tile_pool(name="work", bufs=2))
        psum = ctx.enter_context(tc.psum_pool(name="psum", bufs=1))

        ident = keep.tile([P, P], F32, name="ident")
        make_identity(nc, ident[:])
        warm = keep.tile([P, 2], F32, name="warm")
        nc.vector.memset(warm[:], 0.0)
        nc.scalar.copy(out=warm[:, 0:1], in_=warm[:, 1:2])

        ctx.enter_context(tc.manual_schedule())

        err_sb = keep.tile([P, GROUPS, PACK, X], BF16, name="err_sb", align_bytes=64)
        e1 = keep.tile([P, GROUPS, PACK, X], F32, name="e1", align_bytes=64)
        r_raw = keep.tile([P, GROUPS, PACK], BF16, name="r_raw")
        r_col = keep.tile([P, TILES], F32, name="r_col")
        col = keep.tile([P, X], BF16, name="col", align_bytes=64)
        out_v = out.rearrange("(g p t) x -> g p t x", p=P, t=PACK)
        coarse_v = coarse.rearrange("(g p t) k -> g p t k", p=P, t=PACK)
        err_v = err.rearrange("(g p t) x -> g p t x", p=P, t=PACK)

        def load_weight(w, name):
            raw = work.tile([P, PACK, X], BF16, name=name, tag="raw", bufs=16, align_bytes=64)
            nc.sync.dma_start(out=raw[:], in_=w.rearrange("(p j) n -> p j n", j=PACK))
            return raw

        raws = []

        def load_coarse(i):
            raw = work.tile([P, Y], BF16, name="raw", tag="raw", bufs=16, align_bytes=64)
            nc.sync.dma_start(out=raw[:], in_=coarse_v[i // PACK, :, i % PACK])
            raws.append(raw)

        nc.sync.dma_start(out=err_sb[:, 0, 0:2], in_=err_v[0, :, 0:2])
        pre_raw = load_weight(pre, "pre_raw")
        nc.sync.dma_start(out=err_sb[:, 0, 2:4], in_=err_v[0, :, 2:4])
        nc.sync.dma_start(out=err_sb[:, 1], in_=err_v[1])
        load_coarse(0)
        nc.sync.dma_start(out=err_sb[:, 2], in_=err_v[2])
        load_coarse(1)
        nc.sync.dma_start(out=err_sb[:, 3], in_=err_v[3])
        load_coarse(2)
        load_coarse(3)
        nc.sync.dma_start(out=r_raw[:], in_=row_unscale.rearrange("(g p t) -> p g t", p=P, t=PACK))
        load_coarse(4)
        post_raw = load_weight(post, "post_raw")
        load_coarse(5)
        load_coarse(6)
        load_coarse(7)
        nc.sync.dma_start(out=col[:], in_=col_unscale.partition_broadcast(P))
        load_coarse(8)
        load_coarse(9)
        load_coarse(10)
        load_coarse(11)
        load_coarse(12)
        load_coarse(13)


        def bank_tile(tag):
            bank = psum.tile([P, X], F32, name=tag, tag=tag, bufs=1)
            return bank

        nsort = lambda i: 2 if i > 2 else 0
        tr = {}
        il = {}
        srt = {}
        q = {}
        acc = {}
        d = {}
        e2b = {}
        e3 = {}
        state = {"p1": 0, "p3": 0, "late": 14}

        def new_codes(tag, bufs, width):
            codes = work.tile([P, width], U32, name=tag + "_c", tag=tag + "_c", bufs=bufs, align_bytes=64)
            scales = work.tile([P, width], U8, name=tag + "_s", tag=tag + "_s", bufs=bufs, align_bytes=64)
            return codes, scales

        def quantise(src, dst, lo, hi):
            nc.vector.quantize_mx(out=dst[0][:, lo:hi].bitcast(FP8X4), scales=dst[1][:, lo:hi], in_=src[:, PACK * lo : PACK * hi])

        def mx(out_ap, left, lcol, right, start, stop):
            nc.tensor.matmul_mx(
                out=out_ap,
                lhsT=left[0][:, lcol : lcol + P].bitcast(FP8X4),
                lhsT_scale=left[1][:, lcol : lcol + P],
                rhs=right[0][:].bitcast(FP8X4),
                rhs_scale=right[1][:],
                start=start,
                stop=stop,
            )

        def turn(key, words):
            bank = psum.tile([P, 2, 2, P], F32, name="tr", tag="tr", bufs=3)
            for c in range(2):
                for u in range(2):
                    nc.tensor.transpose(bank[:, c, u, :], words(c, u), ident[:])
            tr[key] = bank

        def untangle(key, il_key, b, copy):
            if il_key not in il:
                il[il_key] = work.tile([P, WIDE], BF16, name="il", tag="il", bufs=7, align_bytes=64)
            dst = il[il_key][:].bitcast(F32).rearrange("p (c m u) -> p c m u", c=PACK, u=2)
            copy(out=dst[:, 2 * b : 2 * b + 2], in_=tr[key][:].rearrange("p c u m -> p c m u"))

        def weave(key, raw, lo, hi, copy):
            if key not in il:
                il[key] = work.tile([P, WIDE], BF16, name="il", tag="il", bufs=7, align_bytes=64)
            copy(
                out=il[key][:].rearrange("p (n j) -> p n j", j=PACK)[:, lo:hi],
                in_=raw[:].rearrange("p j n -> p n j")[:, lo:hi],
            )

        def weave_e1(g, lo, hi, copy):
            key = "e1", g
            if key not in il:
                il[key] = work.tile([P, WIDE], BF16, name="e1il", tag="e1il", bufs=2, align_bytes=64)
            copy(
                out=il[key][:].rearrange("p (x t) -> p x t", t=PACK)[:, lo:hi],
                in_=e1[:, g].rearrange("p t x -> p x t")[:, lo:hi],
            )

        def step(tok):
            k = tok.split()
            n = [int(v) for v in k[1:]]
            k = k[0]
            i = n[0] if n else 0
            if k == "E":
                w = err_sb[:, i].rearrange("p t x -> p (t x)").bitcast(F32)
                turn(("e", i, n[1]), lambda c, u: w[:, 512 * n[1] + 256 * c + u : 512 * n[1] + 256 * (c + 1) : 2])
            elif k == "e":
                untangle(("e", i, n[1]), ("e", i), n[1], nc.scalar.copy)
            elif k == "C":
                w = raws[i][:].bitcast(F32)
                first = PACK - nsort(i)

                def words(c, u):
                    c = 2 * n[1] + c
                    if c < first:
                        return w[:, 256 * c + u : 256 * (c + 1) : 2]
                    s = srt[i][:].bitcast(F32)
                    return s[:, 256 * (c - first) + P * u : 256 * (c - first) + P * (u + 1)]

                turn(("c", i, n[1]), words)
            elif k == "c":
                untangle(("c", i, n[1]), ("c", i), n[1], nc.scalar.copy)
            elif k == "cv":
                untangle(("c", i, n[1]), ("c", i), n[1], nc.vector.tensor_copy)
            elif k == "s":
                m = nsort(i)
                lo = K_PASS * (PACK - m)
                srt[i] = work.tile([P, K_PASS * m], BF16, name="srt", tag="srt", bufs=3, align_bytes=64)
                nc.scalar.copy(
                    out=srt[i][:].bitcast(F32).rearrange("p (c u k) -> p c u k", c=m, u=2),
                    in_=raws[i][:, lo:Y].bitcast(F32).rearrange("p (c k u) -> p c u k", c=m, u=2),
                )
            elif k == "wV":
                weave("pre", pre_raw, 0, 320, nc.vector.tensor_copy)
            elif k == "wS":
                weave("pre", pre_raw, 320, X, nc.scalar.copy)
            elif k == "pre":
                q["pre"] = new_codes("pre", 1, 512)
                quantise(il["pre"], q["pre"], 0, 512)
            elif k == "wp":
                weave("post", post_raw, 0, X, nc.vector.tensor_copy)
            elif k == "postq":
                q["post"] = new_codes("post", 1, 512)
                quantise(il["post"], q["post"], 0, 512)
            elif k == "h":
                if ("e", i) not in q:
                    q["e", i] = new_codes("err", 2, 512)
                if i < 2:
                    quantise(il["e", i], q["e", i], 256 * n[1], 256 * (n[1] + 1))
                else:
                    quantise(il["e", i], q["e", i], 0, 512)
            elif k == "P":
                bank = bank_tile(["e2t", "acc2", "acc3"][state["p1"] % 3])
                state["p1"] += 1
                mx(bank[:], q["e", i], n[1] * P, q["pre"], True, True)
                acc["e", i, n[1]] = bank
            elif k == "t":
                nc.vector.tensor_tensor(out=e1[:, i, n[1]], in0=err_sb[:, i, n[1]], in1=acc["e", i, n[1]][:], op=ALU.subtract)
            elif k == "iS":
                weave_e1(i, 0, 448 if i < 3 else 192, nc.scalar.copy)
            elif k == "iV":
                weave_e1(i, 448 if i < 3 else 192, X, nc.vector.tensor_copy)
            elif k == "q1":
                q["1", i] = new_codes("e1%d" % i, 1, 512)
                quantise(il["e1", i], q["1", i], 0, 512)
            elif k == "R":
                nc.vector.tensor_copy(out=r_col[:], in_=r_raw[:].rearrange("p g t -> p (g t)"))
            elif k == "qc":
                q["c", i] = new_codes("cq", 4, 512)
                quantise(il["c", i], q["c", i], 0, 512)
            elif k == "2":
                if n[1] == 0:
                    acc[i] = bank_tile("acc%d" % (i % 2))
                mx(acc[i][:], q["c", i], n[1] * P, q["1", n[1]], n[1] == 0, n[1] == 3)
            elif k == "d":
                d[i] = work.tile([P, X], F32, name="d", tag="d", bufs=6, align_bytes=64)
                nc.vector.tensor_tensor(out=d[i][:], in0=e1[:, i // PACK, i % PACK], in1=acc[i][:], op=ALU.subtract)
            elif k == "b":
                e2b[i] = work.tile([P, X], BF16, name="e2b", tag="e2b", bufs=3, align_bytes=64)
                nc.scalar.activation(
                    out=e2b[i][:].rearrange("m (u p e) -> m u p e", u=2, e=2),
                    in_=d[i][:].rearrange("m (p u e) -> m u p e", u=2, e=2),
                    func=ACT.Copy,
                    scale=r_col[:, i : i + 1],
                )
            elif k == "T":
                bank = bank_tile("e2t")
                w = e2b[i][:].bitcast(F32)
                for u in range(2):
                    nc.tensor.transpose(bank[:, u * P : (u + 1) * P], w[:, u * P : (u + 1) * P], ident[:])
                tr["e2", i] = bank
            elif k == "x":
                il["e2", i] = work.tile([P, X], BF16, name="e2il", tag="e2il", bufs=2, align_bytes=64)
                nc.scalar.copy(
                    out=il["e2", i][:].bitcast(F32).rearrange("p (m u) -> p m u", u=2),
                    in_=tr["e2", i][:, 0 : 2 * P].rearrange("p (u m) -> p m u", u=2),
                )
            elif k == "y":
                q["e2", i] = new_codes("e2", 3, P)
                quantise(il["e2", i], q["e2", i], 0, P)
            elif k == "3":
                acc["3", i] = bank_tile("acc%d" % (2 + i % 2))
                mx(acc["3", i][:], q["e2", i], 0, q["post"], True, True)
            elif k == "z":
                e3[i] = work.tile([P, X], F32, name="e3", tag="e3", bufs=3, align_bytes=64)
                nc.vector.scalar_tensor_tensor(
                    out=e3[i][:], in0=d[i][:], scalar=r_col[:, i : i + 1], in1=acc["3", i][:], op0=ALU.mult, op1=ALU.subtract
                )
            elif k in ("f", "fp"):
                res = work.tile([P, X], F32, name="res", tag="res", bufs=4, align_bytes=64)
                eng = nc.vector if k == "f" else nc.gpsimd
                eng.tensor_tensor(out=res[:], in0=e3[i][:], in1=col[:], op=ALU.mult)
                nc.sync.dma_start(out=out_v[i // PACK, :, i % PACK], in_=res[:])
            elif k == "L":
                load_coarse(i)
            else:
                raise AssertionError(tok)

        for line in [
            "E 0 0, wV, wS, L 14, E 0 1, e 0 0, e 0 1, E 1 1, h 0 0, h 0 1",
            "E 1 0, pre, e 1 1, h 1 1, P 0 0, e 1 0, P 0 1, t 0 0, P 0 3, h 1 0",
            "t 0 1, P 0 2, E 2 1, t 0 2, t 0 3, E 2 0, e 2 1, iV 0, P 1 3, e 2 0",
            "P 1 2, t 1 3, C 0 1, iS 0, h 2 0, P 1 1, t 1 2, P 1 0, C 0 0, L 15",
            "t 1 1, P 2 1, t 1 0, c 0 0, P 2 3, E 3 0, t 2 1, c 0 1, q1 0, E 3 1",
            "e 3 0, qc 0, P 2 0, e 3 1, C 1 1, t 2 3, iS 1, h 3 0, P 2 2, 2 0 0",
            "t 2 0, P 3 3, iV 1, P 3 2, t 2 2, C 1 0, t 3 3, c 1 1, C 2 0, t 3 2",
            "c 1 0, P 3 1, q1 1, iS 2, P 3 0, C 2 1, t 3 1, 2 0 1, t 3 0, R",
            "qc 1, iS 3, iV 2, iV 3, 2 1 0, 2 1 1, c 2 1, q1 2, c 2 0, q1 3",
            "2 1 2, s 3, 2 0 2, 2 0 3, s 4, 2 1 3, d 0, C 3 1, C 3 0, qc 2",
            "b 0, C 4 1, d 1, c 3 1, T 0, 2 2 0, c 3 0, 2 2 1, x 0, qc 3",
            "2 2 2, s 5, 2 2 3, wp, b 1, C 4 0, c 4 1, C 5 1, postq, c 4 0",
            "T 1, 2 3 0, y 0, x 1, d 2, 2 3 1, s 6, 2 3 2, qc 4, 2 3 3",
            "b 2, 3 0, y 1, C 5 0, d 3, c 5 1, z 0, C 6 1, c 5 0, T 2",
            "2 4 0, x 2, qc 5, 2 4 1, s 7, 2 4 2, y 2, 2 4 3, b 3, 3 1",
            "d 4, C 6 0, c 6 1, z 1, C 7 1, c 6 0, T 3, f 0, 2 5 0, x 3",
            "2 5 1, qc 6, s 8, 2 5 2, 2 5 3, y 3, b 4, 3 2, d 5, C 7 0",
            "c 7 1, z 2, C 8 1, c 7 0, T 4, f 1, 2 6 0, x 4, 2 6 1, qc 7",
            "s 9, 2 6 2, 2 6 3, y 4, b 5, 3 3, d 6, C 8 0, c 8 1, z 3",
            "C 9 1, c 8 0, T 5, f 2, 2 7 0, x 5, 2 7 1, qc 8, s 10, 2 7 2",
            "2 7 3, y 5, b 6, 3 4, d 7, C 9 0, c 9 1, z 4, C 10 1, c 9 0",
            "T 6, f 3, 2 8 0, x 6, 2 8 1, qc 9, s 11, 2 8 2, 2 8 3, y 6",
            "b 7, 3 5, d 8, C 10 0, c 10 1, z 5, C 11 1, c 10 0, T 7, f 4",
            "2 9 0, x 7, 2 9 1, qc 10, s 12, 2 9 2, 2 9 3, y 7, b 8, 3 6",
            "d 9, C 11 0, c 11 1, z 6, C 12 1, c 11 0, T 8, f 5, 2 10 0, x 8",
            "2 10 1, qc 11, s 13, 2 10 2, 2 10 3, y 8, b 9, 3 7, d 10, C 12 0",
            "c 12 1, z 7, C 13 1, c 12 0, T 9, f 6, 2 11 0, x 9, 2 11 1, qc 12",
            "s 14, 2 11 2, 2 11 3, y 9, b 10, 3 8, d 11, C 13 0, c 13 1, z 8",
            "C 14 1, c 13 0, T 10, f 7, 2 12 0, x 10, 2 12 1, qc 13, s 15, 2 12 2",
            "2 12 3, y 10, b 11, 3 9, d 12, C 14 0, c 14 1, z 9, C 15 1, c 14 0",
            "T 11, f 8, 2 13 0, x 11, 2 13 1, qc 14, b 12, 2 13 2, 2 13 3, y 11",
            "c 15 1, 3 10, d 13, C 15 0, z 10, T 12, c 15 0, 2 14 0, f 9, 2 14 1",
            "x 12, 2 14 2, qc 15, b 13, 2 14 3, 3 11, y 12, d 14, T 13, 2 15 0",
            "z 11, x 13, 2 15 1, b 14, 2 15 2, f 10, 2 15 3, 3 12, y 13, d 15",
            "T 14, 3 13, x 14, z 12, b 15, f 11, T 15, y 14, z 13, 3 14",
            "x 15, f 12, y 15, z 14, 3 15, f 13, z 15, f 14, f 15",
        ]:
            for tok in line.split(", "):
                step(tok)
